import numpy as np
import ml_dtypes


def mxq(x, axis, fmt="e4m3"):
    dtype, down = {"e4m3": (ml_dtypes.float8_e4m3fn, 7), "e5m2": (ml_dtypes.float8_e5m2, 14)}[fmt]
    v = np.moveaxis(np.asarray(x, np.float32).astype(ml_dtypes.bfloat16).astype(np.float64), axis, -1)
    blocks = v.reshape(v.shape[:-1] + (-1, 32))
    amax = np.abs(blocks).max(-1, keepdims=True)
    byte = np.maximum(np.where(amax > 0, np.frexp(amax)[1] - 1 + 127, 0) - down, 1)
    scale = np.exp2(byte - 127.0)
    codes = (blocks / scale).astype(np.float32).astype(dtype).astype(np.float64)
    return np.moveaxis((codes * scale).reshape(v.shape), -1, axis)


WIDE = False


def mx_kscale(k):
    if not WIDE:
        return np.ones(k)
    levels = np.array([10, -10, 5, -5, 0])
    if k % 512:
        return np.exp2(np.random.permutation(np.resize(levels, k // 32))).repeat(32)
    a = np.empty((k // 512, 16))
    for p in range(k // 512):
        a[p, :8] = np.random.permutation(np.resize(levels, 8))
        for g in range(8):
            far = levels[np.abs(levels - a[p, g]) >= 10]
            a[p, g + 8] = far[np.random.randint(len(far))]
    return np.exp2(a.ravel()).repeat(32)


def f64(x):
    return np.asarray(x).astype(np.float64)


def striped8(idx):
    return np.concatenate([x.reshape(-1, 16).T for x in idx]).astype(np.uint16)


def runs(offs, k):
    lists = np.stack([offs[16 * r : 16 * r + 16].T.reshape(-1) for r in range(8)]).astype(np.int64)
    return lists[np.arange(k) % 512 // 64]


def pack_weight(w):
    k, n = w.shape
    w = f64(np.asarray(w, np.float32).astype(ml_dtypes.bfloat16)).reshape(k // 32, 32, n)
    amax = np.abs(w).max(1)
    byte = np.clip(np.where(amax > 0, np.frexp(amax)[1] - 1 + 127 - 7, 1), 1, 254)
    scaled = (w * np.exp2(127.0 - byte)[:, None, :]).reshape(k, n).astype(np.float32)
    words = np.ascontiguousarray(scaled.reshape(k // 512, 128, 4, n).transpose(0, 1, 3, 2)).astype(ml_dtypes.float8_e4m3fn).view(np.uint8)
    return words, np.ascontiguousarray(byte.astype(np.uint8).reshape(k // 512, 16, n))


def unpack_weight(words, scales):
    g, p, n, _ = words.shape
    vals = np.ascontiguousarray(words).view(ml_dtypes.float8_e4m3fn).astype(np.float64) * np.repeat(np.exp2(scales.astype(np.float64) - 127.0), 8, axis=1)[..., None]
    return vals.transpose(0, 1, 3, 2).reshape(g * 512, n)


K, T, S, N, H, U = 512, 2048, 512, 512, 512, 512


def setup_inputs():
    n = np.random.standard_normal
    s = mx_kscale(K)[:, None]
    u = mx_kscale(H)
    packed_xT = pack_weight(n((K, T)) * s)
    return {
        "x_words": packed_xT[0],
        "x_scales": packed_xT[1],
        "w1": (n((K, H)) / np.sqrt(K) / s).astype(np.float32),
        "tab": n((H, U)).astype(np.float32),
        "gn": (np.random.uniform(0.5, 1.5, (H, 1)) * u[:, None]).astype(np.float32),
        "w2": (n((H, N)) / np.sqrt(H) / u[:, None]).astype(np.float32),
        "offs": striped8(np.random.randint(0, T, (8, S))),
        "kind": striped8(np.random.randint(0, U, (8, S))),
        "n1": striped8(np.stack([np.random.permutation(S) for _ in range(8)])),
        "n2": striped8(np.stack([np.random.permutation(S) for _ in range(8)])),
    }


def reference(x_words, x_scales, w1, tab, gn, w2, offs, kind, n1, n2):
    xq = unpack_weight(x_words, x_scales)[np.arange(K)[:, None], runs(offs, K)]
    y = mxq(f64(w1), 0, "e4m3").T @ xq
    bx = y + f64(tab)[np.arange(H)[:, None], runs(kind, H)]
    z = f64(gn) * (np.maximum(bx, np.minimum(bx[np.arange(H)[:, None], runs(n1, H)], bx[np.arange(H)[:, None], runs(n2, H)])))
    return mxq(f64(w2), 0, "e4m3").T @ mxq(z, 0, "e4m3")

@@ -1,0 +1,201 @@
+from contextlib import ExitStack
+
+import concourse.mybir as mybir
+
+K, T, S, N, H, U = 512, 2048, 512, 512, 512, 512
+FLOPS = 2 * K * H * S + 2 * H * N * S
+
+F32 = mybir.dt.float32
+BF16 = mybir.dt.bfloat16
+I32 = mybir.dt.int32
+U32 = mybir.dt.uint32
+U16 = mybir.dt.uint16
+U8 = mybir.dt.uint8
+FP8X4 = mybir.dt.float8_e4m3fn_x4
+ALU = mybir.AluOpType
+ACT = mybir.ActivationFunctionType
+
+P = 128
+PACK = 4
+GROUP = 16
+HALF = 256
+CHUNKS = ((0, 256), (256, 256))
+
+
+def tile_picked_hashkind_none_p_kernel(
+    tc, x_words, x_scales, w1, tab, gn, w2, offs, kind, n1, n2, out
+):
+    nc = tc.nc
+    with ExitStack() as ctx:
+        lists = ctx.enter_context(tc.tile_pool(name="lists", bufs=1))
+        keep = ctx.enter_context(tc.tile_pool(name="keep", bufs=1))
+        psum = ctx.enter_context(tc.psum_pool(name="psum", bufs=1))
+
+        def entries(tile, start, count):
+            return tile[:, start // GROUP : (start + count) // GROUP]
+
+        offs_sb = lists.tile([P, S // GROUP], U16, name="offs_sb")
+        kind_sb = lists.tile([P, S // GROUP], U16, name="kind_sb")
+        n1_sb = lists.tile([P, S // GROUP], U16, name="n1_sb")
+        n2_sb = lists.tile([P, S // GROUP], U16, name="n2_sb")
+
+        xs_win = keep.tile([P, T], U8, name="xs_win", align_bytes=64)
+        nc.vector.memset(xs_win[:].bitcast(I32), 0)
+
+        nc.scalar.dma_start(xs_win[0:P:8, :].bitcast(I32), x_scales[0].bitcast(I32))
+        gain = keep.tile([P, PACK], F32, name="gain")
+        nc.gpsimd.dma_start(gain[:], gn.rearrange("(p t) o -> p (t o)", t=PACK))
+        nc.sync.dma_start(offs_sb[:], offs)
+        nc.sync.dma_start(kind_sb[:], kind)
+        nc.sync.dma_start(n1_sb[:], n1)
+        nc.sync.dma_start(n2_sb[:], n2)
+        w1_raw = keep.tile([P, PACK, H], F32, name="w1_raw", tag="w_raw")
+        nc.sync.dma_start(w1_raw[:], w1.rearrange("(p j) c -> p j c", j=PACK))
+        xw_win = keep.tile([P, T], U32, name="xw_win", align_bytes=64)
+        nc.sync.dma_start(xw_win[:].bitcast(I32), x_words[0].rearrange("p n t -> p (n t)").bitcast(I32))
+        tab_planes = tab.rearrange("(p t) c -> t p c", t=PACK)
+        tab_win = []
+        for t in range(PACK):
+            win = keep.tile([P, U], F32, name=f"tab_win{t}")
+            nc.sync.dma_start(win[:], tab_planes[t])
+            tab_win.append(win)
+
+        gain_abs = keep.tile([P, PACK], F32, name="gain_abs")
+        nc.scalar.activation(gain_abs[:], gain[:], ACT.Abs)
+        twice_nonneg = keep.tile([P, PACK], F32, name="twice_nonneg")
+        gain_sign = keep.tile([P, PACK], F32, name="gain_sign")
+        nc.gpsimd.tensor_scalar(twice_nonneg[:], gain[:], 0.0, 2.0, ALU.is_ge, ALU.mult)
+        nc.gpsimd.tensor_scalar(gain_sign[:], twice_nonneg[:], 1.0, -1.0, ALU.mult, ALU.add)
+
+        xs_picked = keep.tile([P, S], U8, name="xs_picked", align_bytes=64)
+        nc.vector.tensor_copy(xs_picked[:], xs_win[:].indirect(offs_sb[:]))
+        xs_plane = keep.tile([P, S], U8, name="xs_plane", align_bytes=64)
+        nc.vector.tensor_copy(xs_plane[:].bitcast(I32), xs_picked[:].bitcast(I32))
+        for r in range(1, 4):
+            nc.scalar.dma_start(xs_plane[r:P:32, :].bitcast(I32), xs_picked[8 * r : P : 32, :].bitcast(I32))
+
+        w1_codes = keep.tile([P, H], U32, name="w1_codes", align_bytes=64)
+        w1_scales = keep.tile([P, H], U8, name="w1_scales", align_bytes=64)
+        w1_view = w1_raw[:].rearrange("p j (m t) -> p m t j", t=PACK)
+        for pair in range(2):
+            grouped = keep.tile([P, 2, P, PACK], BF16, name=f"w1_grouped{pair}", align_bytes=64)
+            dst = grouped[:].rearrange("p t m j -> p m t j")
+            src = w1_view[:, :, 2 * pair : 2 * pair + 2, :]
+            if pair == 0:
+                nc.vector.tensor_copy(dst, src)
+            else:
+                nc.scalar.copy(dst, src)
+            cols = slice(2 * P * pair, 2 * P * (pair + 1))
+            nc.vector.quantize_mx(
+                out=w1_codes[:, cols].bitcast(FP8X4),
+                scales=w1_scales[:, cols],
+                in_=grouped[:].rearrange("p t m j -> p (t m j)"),
+            )
+
+        w2_raw = keep.tile([P, PACK, N], F32, name="w2_raw", tag="w_raw")
+        nc.sync.dma_start(w2_raw[:], w2.rearrange("(p j) c -> p j c", j=PACK))
+
+        xw_picked = []
+        for h in range(2):
+            picked = keep.tile([P, HALF], U32, name=f"xw_picked{h}", align_bytes=64)
+            nc.vector.tensor_copy(picked[:], xw_win[:].indirect(entries(offs_sb, h * HALF, HALF)))
+            xw_picked.append(picked)
+
+        scaled = []
+        rounded = keep.tile([P, PACK, S], BF16, name="rounded", align_bytes=64)
+        for pair in range(2):
+            shifted = [keep.tile([P, S], F32, name=f"shifted{2 * pair + u}") for u in range(2)]
+            for h in range(2):
+                bank = psum.tile([P, 2, HALF], F32, name=f"y_bank{pair}{h}")
+                for u in range(2):
+                    cols = slice(P * (2 * pair + u), P * (2 * pair + u + 1))
+                    nc.tensor.matmul_mx(
+                        out=bank[:, u, :],
+                        lhsT=w1_codes[:, cols].bitcast(FP8X4),
+                        lhsT_scale=w1_scales[:, cols],
+                        rhs=xw_picked[h][:].bitcast(FP8X4),
+                        rhs_scale=xs_plane[:, h * HALF : (h + 1) * HALF],
+                        start=True,
+                        stop=True,
+                    )
+                y = keep.tile([P, 2, HALF], F32, name=f"y{pair}{h}")
+                nc.scalar.copy(y[:], bank[:])
+                for u in range(2):
+                    nc.vector.tensor_tensor(
+                        shifted[u][:, h * HALF : (h + 1) * HALF],
+                        tab_win[2 * pair + u][:].indirect(entries(kind_sb, h * HALF, HALF)),
+                        y[:, u, :],
+                        ALU.add,
+                    )
+            for u in range(2):
+                t = 2 * pair + u
+                win = keep.tile([P, S], F32, name=f"scaled{t}")
+                nc.scalar.activation(win[:], shifted[u][:], ACT.Copy, scale=gain_abs[:, t : t + 1])
+                scaled.append(win)
+        for t in range(PACK):
+            nc.scalar.copy(rounded[:, t, :], scaled[t][:])
+
+        w2_signed = keep.tile([P, PACK, N], BF16, name="w2_signed", tag="bf16_stage", align_bytes=64)
+        for t in range(PACK):
+            nc.scalar.activation(w2_signed[:, t, :], w2_raw[:, t, :], ACT.Copy, scale=gain_sign[:, t : t + 1])
+        w2_grouped = keep.tile([P, N, PACK], BF16, name="w2_grouped", align_bytes=64)
+        nc.scalar.copy(
+            w2_grouped[:].rearrange("p (c i) t -> p c t i", i=4),
+            w2_signed[:].rearrange("p t (c i) -> p c t i", i=4),
+        )
+        w2_codes = keep.tile([P, N], U32, name="w2_codes", align_bytes=64)
+        w2_scales = keep.tile([P, N], U8, name="w2_scales", align_bytes=64)
+        nc.vector.quantize_mx(
+            out=w2_codes[:].bitcast(FP8X4), scales=w2_scales[:], in_=w2_grouped[:].rearrange("p n t -> p (n t)")
+        )
+
+        out_view = out.rearrange("(a p) j -> p a j", p=P)
+        for c, (start, count) in enumerate(CHUNKS):
+            last = c == len(CHUNKS) - 1
+            first_nb = keep.tile([P, PACK, count], BF16, name=f"first_nb{c}", align_bytes=64)
+            second_nb = keep.tile(
+                [P, PACK, count], BF16, name=f"second_nb{c}", tag="bf16_stage" if last else "nb_first", align_bytes=64
+            )
+            for t in range(PACK):
+                nc.vector.tensor_copy(first_nb[:, t, :], scaled[t][:].indirect(entries(n1_sb, start, count)))
+                if not last:
+                    nc.vector.tensor_copy(second_nb[:, t, :], scaled[t][:].indirect(entries(n2_sb, start, count)))
+            for t in range(PACK if last else 0):
+                nc.vector.tensor_copy(second_nb[:, t, :], scaled[t][:].indirect(entries(n2_sb, start, count)))
+            smaller = keep.tile([P, PACK, count], BF16, name=f"smaller{c}", align_bytes=64)
+            nc.vector.tensor_tensor(smaller[:], first_nb[:], second_nb[:], ALU.min)
+            z_planes = keep.tile([P, PACK, count], BF16, name=f"z_planes{c}", align_bytes=64)
+            nc.vector.tensor_tensor(z_planes[:], smaller[:], rounded[:, :, start : start + count], ALU.max)
+            z_grouped = keep.tile(
+                [P, count, PACK], BF16, name=f"z_grouped{c}", tag=f"z_last" if last else "bf16_stage", align_bytes=64
+            )
+            dst = z_grouped[:].rearrange("p (c i) t -> p c t i", i=4)
+            src = z_planes[:].rearrange("p t (c i) -> p c t i", i=4)
+            if last:
+                nc.vector.tensor_copy(dst, src)
+            else:
+                nc.scalar.copy(dst, src)
+            z_codes = keep.tile([P, count], U32, name=f"z_codes{c}", align_bytes=64)
+            z_scales = keep.tile([P, count], U8, name=f"z_scales{c}", align_bytes=64)
+            nc.vector.quantize_mx(
+                out=z_codes[:].bitcast(FP8X4), scales=z_scales[:], in_=z_grouped[:].rearrange("p n t -> p (n t)")
+            )
+            for pair in range(2):
+                bank = psum.tile([P, 2, count], F32, name=f"out_bank{c}{pair}")
+                for u in range(2):
+                    cols = slice(P * (2 * pair + u), P * (2 * pair + u + 1))
+                    nc.tensor.matmul_mx(
+                        out=bank[:, u, :],
+                        lhsT=w2_codes[:, cols].bitcast(FP8X4),
+                        lhsT_scale=w2_scales[:, cols],
+                        rhs=z_codes[:].bitcast(FP8X4),
+                        rhs_scale=z_scales[:],
+                        start=True,
+                        stop=True,
+                    )
+                result = keep.tile([P, 2, count], F32, name=f"result{c}{pair}")
+                if last and pair == 1:
+                    nc.vector.tensor_copy(result[:], bank[:])
+                else:
+                    nc.scalar.copy(result[:], bank[:])
+                nc.sync.dma_start(out_view[:, 2 * pair : 2 * pair + 2, start : start + count], result[:])

@@ -19,7 +19,7 @@ P = 128
 PACK = 4
 GROUP = 16
 HALF = 256
-CHUNKS = ((0, 256), (256, 256))
+CHUNKS = ((0, 256), (256, 128), (384, 128))
 
 
 def tile_picked_hashkind_none_p_kernel(
@@ -40,12 +40,15 @@ def tile_picked_hashkind_none_p_kernel(
         n2_sb = lists.tile([P, S // GROUP], U16, name="n2_sb")
 
         xs_win = keep.tile([P, T], U8, name="xs_win", align_bytes=64)
-        nc.vector.memset(xs_win[:].bitcast(I32), 0)
 
-        nc.scalar.dma_start(xs_win[0:P:8, :].bitcast(I32), x_scales[0].bitcast(I32))
-        gain = keep.tile([P, PACK], F32, name="gain")
-        nc.gpsimd.dma_start(gain[:], gn.rearrange("(p t) o -> p (t o)", t=PACK))
+        nc.vector.memset(xs_win[:, : T // 2].bitcast(I32), 0)
+        nc.gpsimd.memset(xs_win[:, T // 2 :].bitcast(I32), 0)
+        scale_rows = x_scales[0].bitcast(I32).rearrange("(g e) c -> e g c", e=2)
+        for e in range(2):
+            nc.sync.dma_start(xs_win[e:P:GROUP, :].bitcast(I32), scale_rows[e])
         nc.sync.dma_start(offs_sb[:], offs)
+        gain = keep.tile([P, PACK], F32, name="gain")
+        nc.sync.dma_start(gain[:], gn.rearrange("(p t) o -> p (t o)", t=PACK))
         nc.sync.dma_start(kind_sb[:], kind)
         nc.sync.dma_start(n1_sb[:], n1)
         nc.sync.dma_start(n2_sb[:], n2)
@@ -71,8 +74,8 @@ def tile_picked_hashkind_none_p_kernel(
         nc.vector.tensor_copy(xs_picked[:], xs_win[:].indirect(offs_sb[:]))
         xs_plane = keep.tile([P, S], U8, name="xs_plane", align_bytes=64)
         nc.vector.tensor_copy(xs_plane[:].bitcast(I32), xs_picked[:].bitcast(I32))
-        for r in range(1, 4):
-            nc.scalar.dma_start(xs_plane[r:P:32, :].bitcast(I32), xs_picked[8 * r : P : 32, :].bitcast(I32))
+        for e in range(2):
+            nc.scalar.dma_start(xs_plane[2 + e : P : 32, :].bitcast(I32), xs_picked[GROUP + e : P : 32, :].bitcast(I32))
 
         w1_codes = keep.tile([P, H], U32, name="w1_codes", align_bytes=64)
         w1_scales = keep.tile([P, H], U8, name="w1_scales", align_bytes=64)
@@ -102,9 +105,19 @@ def tile_picked_hashkind_none_p_kernel(
             xw_picked.append(picked)
 
         scaled = []
+        unscaled = []
         rounded = keep.tile([P, PACK, S], BF16, name="rounded", align_bytes=64)
         for pair in range(2):
-            shifted = [keep.tile([P, S], F32, name=f"shifted{2 * pair + u}") for u in range(2)]
+            shifted = [
+                keep.tile(
+                    [P, S],
+                    F32,
+                    name=f"shifted{2 * pair + u}",
+                    tag="bf16_stage" if 2 * pair + u == PACK - 1 else f"shifted{2 * pair + u}",
+                    align_bytes=64,
+                )
+                for u in range(2)
+            ]
             for h in range(2):
                 bank = psum.tile([P, 2, HALF], F32, name=f"y_bank{pair}{h}")
                 for u in range(2):
@@ -132,8 +145,9 @@ def tile_picked_hashkind_none_p_kernel(
                 win = keep.tile([P, S], F32, name=f"scaled{t}")
                 nc.scalar.activation(win[:], shifted[u][:], ACT.Copy, scale=gain_abs[:, t : t + 1])
                 scaled.append(win)
+                unscaled.append(shifted[u])
         for t in range(PACK):
-            nc.scalar.copy(rounded[:, t, :], scaled[t][:])
+            nc.scalar.activation(rounded[:, t, :], unscaled[t][:], ACT.Copy, scale=gain_abs[:, t : t + 1])
 
         w2_signed = keep.tile([P, PACK, N], BF16, name="w2_signed", tag="bf16_stage", align_bytes=64)
         for t in range(PACK):
@@ -150,25 +164,37 @@ def tile_picked_hashkind_none_p_kernel(
         )
 
         out_view = out.rearrange("(a p) j -> p a j", p=P)
+        first_tags = ("first0", "smaller0", "smaller1")
+        grouped_tags = ("bf16_stage", "grouped1", "grouped2")
         for c, (start, count) in enumerate(CHUNKS):
             last = c == len(CHUNKS) - 1
-            first_nb = keep.tile([P, PACK, count], BF16, name=f"first_nb{c}", align_bytes=64)
-            second_nb = keep.tile(
-                [P, PACK, count], BF16, name=f"second_nb{c}", tag="bf16_stage" if last else "nb_first", align_bytes=64
-            )
-            for t in range(PACK):
-                nc.vector.tensor_copy(first_nb[:, t, :], scaled[t][:].indirect(entries(n1_sb, start, count)))
-                if not last:
-                    nc.vector.tensor_copy(second_nb[:, t, :], scaled[t][:].indirect(entries(n2_sb, start, count)))
-            for t in range(PACK if last else 0):
-                nc.vector.tensor_copy(second_nb[:, t, :], scaled[t][:].indirect(entries(n2_sb, start, count)))
+            planes_held = PACK + (2 if last else PACK)
+            both_nb = keep.tile([P, planes_held, count], BF16, name=f"both_nb{c}", tag=first_tags[c], align_bytes=64)
+            first_nb = both_nb[:, :PACK, :]
             smaller = keep.tile([P, PACK, count], BF16, name=f"smaller{c}", align_bytes=64)
-            nc.vector.tensor_tensor(smaller[:], first_nb[:], second_nb[:], ALU.min)
+            if not last:
+                second_nb = both_nb[:, PACK:, :]
+                for t in range(PACK):
+                    nc.vector.tensor_copy(first_nb[:, t, :], scaled[t][:].indirect(entries(n1_sb, start, count)))
+                    nc.vector.tensor_copy(second_nb[:, t, :], scaled[t][:].indirect(entries(n2_sb, start, count)))
+                nc.vector.tensor_tensor(smaller[:], first_nb, second_nb, ALU.min)
+            else:
+                for t in range(PACK):
+                    nc.vector.tensor_copy(first_nb[:, t, :], scaled[t][:].indirect(entries(n1_sb, start, count)))
+                for pair in range(2):
+                    if pair == 0:
+                        second_nb = both_nb[:, PACK:, :]
+                    else:
+                        late_nb = keep.tile([P, 2, count], BF16, name="late_nb", tag=grouped_tags[c - 1], align_bytes=64)
+                        second_nb = late_nb[:]
+                    for u in range(2):
+                        t = 2 * pair + u
+                        nc.vector.tensor_copy(second_nb[:, u, :], scaled[t][:].indirect(entries(n2_sb, start, count)))
+                    planes = slice(2 * pair, 2 * pair + 2)
+                    nc.vector.tensor_tensor(smaller[:, planes, :], first_nb[:, planes, :], second_nb, ALU.min)
             z_planes = keep.tile([P, PACK, count], BF16, name=f"z_planes{c}", align_bytes=64)
             nc.vector.tensor_tensor(z_planes[:], smaller[:], rounded[:, :, start : start + count], ALU.max)
-            z_grouped = keep.tile(
-                [P, count, PACK], BF16, name=f"z_grouped{c}", tag=f"z_last" if last else "bf16_stage", align_bytes=64
-            )
+            z_grouped = keep.tile([P, count, PACK], BF16, name=f"z_grouped{c}", tag=grouped_tags[c], align_bytes=64)
             dst = z_grouped[:].rearrange("p (c i) t -> p c t i", i=4)
             src = z_planes[:].rearrange("p t (c i) -> p c t i", i=4)
             if last:
@@ -181,9 +207,11 @@ def tile_picked_hashkind_none_p_kernel(
                 out=z_codes[:].bitcast(FP8X4), scales=z_scales[:], in_=z_grouped[:].rearrange("p n t -> p (n t)")
             )
             for pair in range(2):
-                bank = psum.tile([P, 2, count], F32, name=f"out_bank{c}{pair}")
+                result = keep.tile([P, 2, count], F32, name=f"result{c}{pair}")
+                bank = psum.tile([P, 2, count], F32, name=f"out_bank{c}{pair}", tag=f"out_bank{c % 2}{pair}")
                 for u in range(2):
-                    cols = slice(P * (2 * pair + u), P * (2 * pair + u + 1))
+                    a = 2 * pair + u
+                    cols = slice(P * a, P * (a + 1))
                     nc.tensor.matmul_mx(
                         out=bank[:, u, :],
                         lhsT=w2_codes[:, cols].bitcast(FP8X4),
@@ -193,7 +221,6 @@ def tile_picked_hashkind_none_p_kernel(
                         start=True,
                         stop=True,
                     )
-                result = keep.tile([P, 2, count], F32, name=f"result{c}{pair}")
                 if last and pair == 1:
                     nc.vector.tensor_copy(result[:], bank[:])
                 else:

@@ -19,7 +19,7 @@ P = 128
 PACK = 4
 GROUP = 16
 HALF = 256
-CHUNKS = ((0, 256), (256, 128), (384, 128))
+CHUNKS = ((0, 256), (256, 256))
 
 
 def tile_picked_hashkind_none_p_kernel(
@@ -29,6 +29,7 @@ def tile_picked_hashkind_none_p_kernel(
     with ExitStack() as ctx:
         lists = ctx.enter_context(tc.tile_pool(name="lists", bufs=1))
         keep = ctx.enter_context(tc.tile_pool(name="keep", bufs=1))
+        stage = ctx.enter_context(tc.tile_pool(name="stage", bufs=1))
         psum = ctx.enter_context(tc.psum_pool(name="psum", bufs=1))
 
         def entries(tile, start, count):
@@ -50,18 +51,12 @@ def tile_picked_hashkind_none_p_kernel(
         gain = keep.tile([P, PACK], F32, name="gain")
         nc.sync.dma_start(gain[:], gn.rearrange("(p t) o -> p (t o)", t=PACK))
         nc.sync.dma_start(kind_sb[:], kind)
+        w1_raw = stage.tile([P, PACK, H], F32, name="w1_raw", offset=0)
+        nc.sync.dma_start(w1_raw[:], w1.rearrange("(p j) c -> p j c", j=PACK))
+        xw_win = keep.tile([P, T], U32, name="xw_win", tag="big_load", align_bytes=64)
+        nc.sync.dma_start(xw_win[:].bitcast(I32), x_words[0].rearrange("p n t -> p (n t)").bitcast(I32))
         nc.sync.dma_start(n1_sb[:], n1)
         nc.sync.dma_start(n2_sb[:], n2)
-        w1_raw = keep.tile([P, PACK, H], F32, name="w1_raw", tag="w_raw")
-        nc.sync.dma_start(w1_raw[:], w1.rearrange("(p j) c -> p j c", j=PACK))
-        xw_win = keep.tile([P, T], U32, name="xw_win", align_bytes=64)
-        nc.sync.dma_start(xw_win[:].bitcast(I32), x_words[0].rearrange("p n t -> p (n t)").bitcast(I32))
-        tab_planes = tab.rearrange("(p t) c -> t p c", t=PACK)
-        tab_win = []
-        for t in range(PACK):
-            win = keep.tile([P, U], F32, name=f"tab_win{t}")
-            nc.sync.dma_start(win[:], tab_planes[t])
-            tab_win.append(win)
 
         gain_abs = keep.tile([P, PACK], F32, name="gain_abs")
         nc.scalar.activation(gain_abs[:], gain[:], ACT.Abs)
@@ -95,8 +90,12 @@ def tile_picked_hashkind_none_p_kernel(
                 in_=grouped[:].rearrange("p t m j -> p (t m j)"),
             )
 
-        w2_raw = keep.tile([P, PACK, N], F32, name="w2_raw", tag="w_raw")
-        nc.sync.dma_start(w2_raw[:], w2.rearrange("(p j) c -> p j c", j=PACK))
+        tab_planes = tab.rearrange("(p t) c -> t p c", t=PACK)
+        tab_win = []
+        for t in range(PACK):
+            win = stage.tile([P, U], F32, name=f"tab_win{t}", offset=4 * U * t)
+            nc.sync.dma_start(win[:], tab_planes[t])
+            tab_win.append(win)
 
         xw_picked = []
         for h in range(2):
@@ -104,26 +103,24 @@ def tile_picked_hashkind_none_p_kernel(
             nc.vector.tensor_copy(picked[:], xw_win[:].indirect(entries(offs_sb, h * HALF, HALF)))
             xw_picked.append(picked)
 
+        w2_raw = keep.tile([P, PACK, N], F32, name="w2_raw", tag="big_load", align_bytes=64)
+        nc.sync.dma_start(w2_raw[:], w2.rearrange("(p j) c -> p j c", j=PACK))
         scaled = []
-        unscaled = []
         rounded = keep.tile([P, PACK, S], BF16, name="rounded", align_bytes=64)
         for pair in range(2):
-            shifted = [
-                keep.tile(
-                    [P, S],
-                    F32,
-                    name=f"shifted{2 * pair + u}",
-                    tag="bf16_stage" if 2 * pair + u == PACK - 1 else f"shifted{2 * pair + u}",
-                    align_bytes=64,
-                )
-                for u in range(2)
-            ]
+            wins = [keep.tile([P, 2 * S], F32, name=f"bx_win{2 * pair + u}") for u in range(2)]
             for h in range(2):
+                y = keep.tile([P, 2, HALF], F32, name=f"y{pair}{h}")
+                first = pair == 0 and h == 0
                 bank = psum.tile([P, 2, HALF], F32, name=f"y_bank{pair}{h}")
+                targets = [bank[:, 0, :], bank[:, 1, :]]
+                if first:
+                    lead_bank = psum.tile([P, HALF], F32, name="lead_bank")
+                    targets[0] = lead_bank[:]
                 for u in range(2):
                     cols = slice(P * (2 * pair + u), P * (2 * pair + u + 1))
                     nc.tensor.matmul_mx(
-                        out=bank[:, u, :],
+                        out=targets[u],
                         lhsT=w1_codes[:, cols].bitcast(FP8X4),
                         lhsT_scale=w1_scales[:, cols],
                         rhs=xw_picked[h][:].bitcast(FP8X4),
@@ -131,25 +128,25 @@ def tile_picked_hashkind_none_p_kernel(
                         start=True,
                         stop=True,
                     )
-                y = keep.tile([P, 2, HALF], F32, name=f"y{pair}{h}")
-                nc.scalar.copy(y[:], bank[:])
+                    if first:
+                        nc.scalar.copy(y[:, u, :], targets[u])
+                if not first:
+                    nc.scalar.copy(y[:], bank[:])
                 for u in range(2):
                     nc.vector.tensor_tensor(
-                        shifted[u][:, h * HALF : (h + 1) * HALF],
+                        wins[u][:, S + h * HALF : S + (h + 1) * HALF],
                         tab_win[2 * pair + u][:].indirect(entries(kind_sb, h * HALF, HALF)),
                         y[:, u, :],
                         ALU.add,
                     )
             for u in range(2):
                 t = 2 * pair + u
-                win = keep.tile([P, S], F32, name=f"scaled{t}")
-                nc.scalar.activation(win[:], shifted[u][:], ACT.Copy, scale=gain_abs[:, t : t + 1])
-                scaled.append(win)
-                unscaled.append(shifted[u])
+                nc.scalar.activation(wins[u][:, :S], wins[u][:, S:], ACT.Copy, scale=gain_abs[:, t : t + 1])
+                scaled.append(wins[u])
         for t in range(PACK):
-            nc.scalar.activation(rounded[:, t, :], unscaled[t][:], ACT.Copy, scale=gain_abs[:, t : t + 1])
+            nc.scalar.copy(rounded[:, t, :], scaled[t][:, :S])
 
-        w2_signed = keep.tile([P, PACK, N], BF16, name="w2_signed", tag="bf16_stage", align_bytes=64)
+        w2_signed = stage.tile([P, PACK, N], BF16, name="w2_signed", offset=4 * U * 2, align_bytes=64)
         for t in range(PACK):
             nc.scalar.activation(w2_signed[:, t, :], w2_raw[:, t, :], ACT.Copy, scale=gain_sign[:, t : t + 1])
         w2_grouped = keep.tile([P, N, PACK], BF16, name="w2_grouped", align_bytes=64)
@@ -164,65 +161,80 @@ def tile_picked_hashkind_none_p_kernel(
         )
 
         out_view = out.rearrange("(a p) j -> p a j", p=P)
-        first_tags = ("first0", "smaller0", "smaller1")
-        grouped_tags = ("bf16_stage", "grouped1", "grouped2")
-        for c, (start, count) in enumerate(CHUNKS):
-            last = c == len(CHUNKS) - 1
-            planes_held = PACK + (2 if last else PACK)
-            both_nb = keep.tile([P, planes_held, count], BF16, name=f"both_nb{c}", tag=first_tags[c], align_bytes=64)
-            first_nb = both_nb[:, :PACK, :]
-            smaller = keep.tile([P, PACK, count], BF16, name=f"smaller{c}", align_bytes=64)
-            if not last:
-                second_nb = both_nb[:, PACK:, :]
-                for t in range(PACK):
-                    nc.vector.tensor_copy(first_nb[:, t, :], scaled[t][:].indirect(entries(n1_sb, start, count)))
-                    nc.vector.tensor_copy(second_nb[:, t, :], scaled[t][:].indirect(entries(n2_sb, start, count)))
-                nc.vector.tensor_tensor(smaller[:], first_nb, second_nb, ALU.min)
-            else:
-                for t in range(PACK):
-                    nc.vector.tensor_copy(first_nb[:, t, :], scaled[t][:].indirect(entries(n1_sb, start, count)))
-                for pair in range(2):
-                    if pair == 0:
-                        second_nb = both_nb[:, PACK:, :]
-                    else:
-                        late_nb = keep.tile([P, 2, count], BF16, name="late_nb", tag=grouped_tags[c - 1], align_bytes=64)
-                        second_nb = late_nb[:]
-                    for u in range(2):
-                        t = 2 * pair + u
-                        nc.vector.tensor_copy(second_nb[:, u, :], scaled[t][:].indirect(entries(n2_sb, start, count)))
-                    planes = slice(2 * pair, 2 * pair + 2)
-                    nc.vector.tensor_tensor(smaller[:, planes, :], first_nb[:, planes, :], second_nb, ALU.min)
-            z_planes = keep.tile([P, PACK, count], BF16, name=f"z_planes{c}", align_bytes=64)
-            nc.vector.tensor_tensor(z_planes[:], smaller[:], rounded[:, :, start : start + count], ALU.max)
-            z_grouped = keep.tile([P, count, PACK], BF16, name=f"z_grouped{c}", tag=grouped_tags[c], align_bytes=64)
-            dst = z_grouped[:].rearrange("p (c i) t -> p c t i", i=4)
-            src = z_planes[:].rearrange("p t (c i) -> p c t i", i=4)
-            if last:
-                nc.vector.tensor_copy(dst, src)
-            else:
-                nc.scalar.copy(dst, src)
-            z_codes = keep.tile([P, count], U32, name=f"z_codes{c}", align_bytes=64)
-            z_scales = keep.tile([P, count], U8, name=f"z_scales{c}", align_bytes=64)
+
+        def quantise(grouped, count, label):
+            codes = keep.tile([P, count], U32, name=f"z_codes{label}", align_bytes=64)
+            scales = keep.tile([P, count], U8, name=f"z_scales{label}", align_bytes=64)
             nc.vector.quantize_mx(
-                out=z_codes[:].bitcast(FP8X4), scales=z_scales[:], in_=z_grouped[:].rearrange("p n t -> p (n t)")
+                out=codes[:].bitcast(FP8X4), scales=scales[:], in_=grouped[:].rearrange("p n t -> p (n t)")
             )
+            return codes, scales
+
+        def second_product(codes, scales, pair, bank):
+            for u in range(2):
+                cols = slice(P * (2 * pair + u), P * (2 * pair + u + 1))
+                nc.tensor.matmul_mx(
+                    out=bank[:, u, :],
+                    lhsT=w2_codes[:, cols].bitcast(FP8X4),
+                    lhsT_scale=w2_scales[:, cols],
+                    rhs=codes[:].bitcast(FP8X4),
+                    rhs_scale=scales[:],
+                    start=True,
+                    stop=True,
+                )
+
+        def interleave_views(grouped, planes):
+            return grouped.rearrange("p (c i) t -> p c t i", i=4), planes.rearrange("p t (c i) -> p c t i", i=4)
+
+        first_nb = keep.tile([P, PACK, S], BF16, name="first_nb", align_bytes=64)
+        for t in range(PACK):
+            nc.vector.tensor_copy(first_nb[:, t, :], scaled[t][:].indirect(n1_sb[:]))
+
+        second_nb = keep.tile([P, PACK, HALF], BF16, name="second_nb", align_bytes=64)
+        for t in range(PACK):
+            nc.vector.tensor_copy(second_nb[:, t, :], scaled[t][:].indirect(entries(n2_sb, 0, HALF)))
+        smaller = keep.tile([P, PACK, HALF], BF16, name="smaller", tag="early_slot", align_bytes=64)
+        nc.vector.tensor_tensor(smaller[:], first_nb[:, :, :HALF], second_nb[:], ALU.min)
+        z_planes = keep.tile([P, PACK, HALF], BF16, name="z_planes", align_bytes=64)
+        nc.vector.tensor_tensor(z_planes[:], smaller[:], rounded[:, :, :HALF], ALU.max)
+        z_grouped = stage.tile([P, HALF, PACK], BF16, name="z_grouped", offset=4 * U * 2, align_bytes=64)
+        nc.scalar.copy(*interleave_views(z_grouped[:], z_planes[:]))
+        codes, scales = quantise(z_grouped, HALF, "early")
+        for pair in range(2):
+            bank = psum.tile([P, 2, HALF], F32, name=f"out_bank{pair}")
+            second_product(codes, scales, pair, bank)
+            result = keep.tile([P, 2, HALF], F32, name=f"result{pair}")
+            nc.scalar.copy(result[:], bank[:])
+            nc.sync.dma_start(out_view[:, 2 * pair : 2 * pair + 2, :HALF], result[:])
+
+        smaller_late = keep.tile([P, PACK, HALF], BF16, name="smaller_late", align_bytes=64)
+        z_late = keep.tile([P, PACK, HALF], BF16, name="z_late", align_bytes=64)
+        for pair in range(2):
+            if pair == 0:
+                nb = keep.tile([P, 2, HALF], BF16, name="late_nb0", tag="early_slot", align_bytes=64)
+            else:
+                nb = stage.tile([P, 2, HALF], BF16, name="late_nb1", offset=4 * U * 2, align_bytes=64)
+            for u in range(2):
+                nc.vector.tensor_copy(nb[:, u, :], scaled[2 * pair + u][:].indirect(entries(n2_sb, HALF, HALF)))
+            planes = slice(2 * pair, 2 * pair + 2)
+            nc.vector.tensor_tensor(smaller_late[:, planes, :], first_nb[:, planes, HALF:], nb[:], ALU.min)
+        nc.vector.tensor_tensor(z_late[:], smaller_late[:], rounded[:, :, HALF:], ALU.max)
+        quarter = HALF // 2
+        for q in range(2):
+            grouped = keep.tile([P, quarter, PACK], BF16, name=f"z_grouped_late{q}", align_bytes=64)
+            views = interleave_views(grouped[:], z_late[:, :, q * quarter : (q + 1) * quarter])
+            if q == 0:
+                nc.vector.tensor_copy(*views)
+            else:
+                nc.scalar.copy(*views)
+            codes, scales = quantise(grouped, quarter, f"late{q}")
+            result = keep.tile([P, PACK, quarter], F32, name=f"result_late{q}")
             for pair in range(2):
-                result = keep.tile([P, 2, count], F32, name=f"result{c}{pair}")
-                bank = psum.tile([P, 2, count], F32, name=f"out_bank{c}{pair}", tag=f"out_bank{c % 2}{pair}")
-                for u in range(2):
-                    a = 2 * pair + u
-                    cols = slice(P * a, P * (a + 1))
-                    nc.tensor.matmul_mx(
-                        out=bank[:, u, :],
-                        lhsT=w2_codes[:, cols].bitcast(FP8X4),
-                        lhsT_scale=w2_scales[:, cols],
-                        rhs=z_codes[:].bitcast(FP8X4),
-                        rhs_scale=z_scales[:],
-                        start=True,
-                        stop=True,
-                    )
-                if last and pair == 1:
-                    nc.vector.tensor_copy(result[:], bank[:])
+                bank = psum.tile([P, 2, quarter], F32, name=f"late_bank{q}{pair}", tag=f"y_bank{q}{pair}")
+                second_product(codes, scales, pair, bank)
+                if pair == 0:
+                    nc.scalar.copy(result[:, :2, :], bank[:])
                 else:
-                    nc.scalar.copy(result[:], bank[:])
-                nc.sync.dma_start(out_view[:, 2 * pair : 2 * pair + 2, start : start + count], result[:])
+                    nc.vector.tensor_copy(result[:, 2:, :], bank[:])
+            start = HALF + q * quarter
+            nc.sync.dma_start(out_view[:, :, start : start + quarter], result[:])

@@ -29,7 +29,6 @@ def tile_picked_hashkind_none_p_kernel(
     with ExitStack() as ctx:
         lists = ctx.enter_context(tc.tile_pool(name="lists", bufs=1))
         keep = ctx.enter_context(tc.tile_pool(name="keep", bufs=1))
-        stage = ctx.enter_context(tc.tile_pool(name="stage", bufs=1))
         psum = ctx.enter_context(tc.psum_pool(name="psum", bufs=1))
 
         def entries(tile, start, count):
@@ -51,7 +50,15 @@ def tile_picked_hashkind_none_p_kernel(
         gain = keep.tile([P, PACK], F32, name="gain")
         nc.sync.dma_start(gain[:], gn.rearrange("(p t) o -> p (t o)", t=PACK))
         nc.sync.dma_start(kind_sb[:], kind)
-        w1_raw = stage.tile([P, PACK, H], F32, name="w1_raw", offset=0)
+        tab_planes = tab.rearrange("(p t) c -> t p c", t=PACK)
+
+        def load_tab(t):
+            win = keep.tile([P, 2 * U], F32, name=f"tab_win{t}")
+            nc.sync.dma_start(win[:, U:], tab_planes[t])
+            return win
+
+        tab_win = [load_tab(t) for t in range(PACK)]
+        w1_raw = keep.tile([P, PACK, H], F32, name="w1_raw")
         nc.sync.dma_start(w1_raw[:], w1.rearrange("(p j) c -> p j c", j=PACK))
         xw_win = keep.tile([P, T], U32, name="xw_win", tag="big_load", align_bytes=64)
         nc.sync.dma_start(xw_win[:].bitcast(I32), x_words[0].rearrange("p n t -> p (n t)").bitcast(I32))
@@ -70,83 +77,65 @@ def tile_picked_hashkind_none_p_kernel(
         xs_plane = keep.tile([P, S], U8, name="xs_plane", align_bytes=64)
         nc.vector.tensor_copy(xs_plane[:].bitcast(I32), xs_picked[:].bitcast(I32))
         for e in range(2):
-            nc.scalar.dma_start(xs_plane[2 + e : P : 32, :].bitcast(I32), xs_picked[GROUP + e : P : 32, :].bitcast(I32))
+            nc.sync.dma_start(xs_plane[2 + e : P : 32, :].bitcast(I32), xs_picked[GROUP + e : P : 32, :].bitcast(I32))
 
-        w1_codes = keep.tile([P, H], U32, name="w1_codes", align_bytes=64)
-        w1_scales = keep.tile([P, H], U8, name="w1_scales", align_bytes=64)
+        bx_win = [keep.tile([P, 2 * S], F32, name=f"bx_win{t}") for t in range(PACK)]
+
+        def pick_shift(t):
+            nc.scalar.activation(tab_win[t][:, :U], tab_win[t][:, U:], ACT.Copy, scale=gain_abs[:, t : t + 1])
+            nc.vector.tensor_copy(bx_win[t][:, S:], tab_win[t][:].indirect(kind_sb[:]))
+
+        for t in range(PACK):
+            pick_shift(t)
+
         w1_view = w1_raw[:].rearrange("p j (m t) -> p m t j", t=PACK)
+        w1_grouped = []
         for pair in range(2):
             grouped = keep.tile([P, 2, P, PACK], BF16, name=f"w1_grouped{pair}", align_bytes=64)
-            dst = grouped[:].rearrange("p t m j -> p m t j")
-            src = w1_view[:, :, 2 * pair : 2 * pair + 2, :]
-            if pair == 0:
-                nc.vector.tensor_copy(dst, src)
-            else:
-                nc.scalar.copy(dst, src)
-            cols = slice(2 * P * pair, 2 * P * (pair + 1))
+            nc.scalar.copy(grouped[:].rearrange("p t m j -> p m t j"), w1_view[:, :, 2 * pair : 2 * pair + 2, :])
+            w1_grouped.append(grouped)
+
+        def quantise_w1(pair, tag):
+            codes = keep.tile([P, 2 * P], U32, name=f"w1_codes{pair}", tag=tag, align_bytes=64)
+            scales = keep.tile([P, 2 * P], U8, name=f"w1_scales{pair}", align_bytes=64)
             nc.vector.quantize_mx(
-                out=w1_codes[:, cols].bitcast(FP8X4),
-                scales=w1_scales[:, cols],
-                in_=grouped[:].rearrange("p t m j -> p (t m j)"),
+                out=codes[:].bitcast(FP8X4), scales=scales[:], in_=w1_grouped[pair][:].rearrange("p t m j -> p (t m j)")
             )
+            return codes, scales
 
-        tab_planes = tab.rearrange("(p t) c -> t p c", t=PACK)
-        tab_win = []
-        for t in range(PACK):
-            win = stage.tile([P, U], F32, name=f"tab_win{t}", offset=4 * U * t)
-            nc.sync.dma_start(win[:], tab_planes[t])
-            tab_win.append(win)
-
-        xw_picked = []
-        for h in range(2):
-            picked = keep.tile([P, HALF], U32, name=f"xw_picked{h}", align_bytes=64)
-            nc.vector.tensor_copy(picked[:], xw_win[:].indirect(entries(offs_sb, h * HALF, HALF)))
-            xw_picked.append(picked)
-
-        w2_raw = keep.tile([P, PACK, N], F32, name="w2_raw", tag="big_load", align_bytes=64)
+        w1_mx = [quantise_w1(0, "w1_codes0")]
+        xw_picked = keep.tile([P, S], U32, name="xw_picked", align_bytes=64)
+        nc.vector.tensor_copy(xw_picked[:], xw_win[:].indirect(offs_sb[:]))
+        w1_mx.append(quantise_w1(1, "big_load"))
+        w2_raw = keep.tile([P, PACK, N], F32, name="w2_raw", tag="xs_picked", align_bytes=64)
         nc.sync.dma_start(w2_raw[:], w2.rearrange("(p j) c -> p j c", j=PACK))
-        scaled = []
+
         rounded = keep.tile([P, PACK, S], BF16, name="rounded", align_bytes=64)
-        for pair in range(2):
-            wins = [keep.tile([P, 2 * S], F32, name=f"bx_win{2 * pair + u}") for u in range(2)]
-            for h in range(2):
-                y = keep.tile([P, 2, HALF], F32, name=f"y{pair}{h}")
-                first = pair == 0 and h == 0
-                bank = psum.tile([P, 2, HALF], F32, name=f"y_bank{pair}{h}")
-                targets = [bank[:, 0, :], bank[:, 1, :]]
-                if first:
-                    lead_bank = psum.tile([P, HALF], F32, name="lead_bank")
-                    targets[0] = lead_bank[:]
-                for u in range(2):
-                    cols = slice(P * (2 * pair + u), P * (2 * pair + u + 1))
-                    nc.tensor.matmul_mx(
-                        out=targets[u],
-                        lhsT=w1_codes[:, cols].bitcast(FP8X4),
-                        lhsT_scale=w1_scales[:, cols],
-                        rhs=xw_picked[h][:].bitcast(FP8X4),
-                        rhs_scale=xs_plane[:, h * HALF : (h + 1) * HALF],
-                        start=True,
-                        stop=True,
-                    )
-                    if first:
-                        nc.scalar.copy(y[:, u, :], targets[u])
-                if not first:
-                    nc.scalar.copy(y[:], bank[:])
-                for u in range(2):
-                    nc.vector.tensor_tensor(
-                        wins[u][:, S + h * HALF : S + (h + 1) * HALF],
-                        tab_win[2 * pair + u][:].indirect(entries(kind_sb, h * HALF, HALF)),
-                        y[:, u, :],
-                        ALU.add,
-                    )
-            for u in range(2):
-                t = 2 * pair + u
-                nc.scalar.activation(wins[u][:, :S], wins[u][:, S:], ACT.Copy, scale=gain_abs[:, t : t + 1])
-                scaled.append(wins[u])
+        for t in range(PACK):
+            bank = psum.tile([P, S], F32, name=f"y_bank{t // 2}{t % 2}")
+            cols = slice(P * (t % 2), P * (t % 2 + 1))
+            nc.tensor.matmul_mx(
+                out=bank[:],
+                lhsT=w1_mx[t // 2][0][:, cols].bitcast(FP8X4),
+                lhsT_scale=w1_mx[t // 2][1][:, cols],
+                rhs=xw_picked[:].bitcast(FP8X4),
+                rhs_scale=xs_plane[:],
+                start=True,
+                stop=True,
+            )
+            if t == 0:
+                nc.vector.scalar_tensor_tensor(
+                    bx_win[t][:, :S], bank[:], gain_abs[:, t : t + 1], bx_win[t][:, S:], ALU.mult, ALU.add
+                )
+            else:
+                y = keep.tile([P, S], F32, name=f"y{t}")
+                nc.scalar.activation(y[:], bank[:], ACT.Copy, scale=gain_abs[:, t : t + 1])
+                nc.gpsimd.tensor_tensor(bx_win[t][:, :S], y[:], bx_win[t][:, S:], ALU.add)
+        scaled = bx_win
         for t in range(PACK):
             nc.scalar.copy(rounded[:, t, :], scaled[t][:, :S])
 
-        w2_signed = stage.tile([P, PACK, N], BF16, name="w2_signed", offset=4 * U * 2, align_bytes=64)
+        w2_signed = keep.tile([P, PACK, N], BF16, name="w2_signed", tag="late_slot", align_bytes=64)
         for t in range(PACK):
             nc.scalar.activation(w2_signed[:, t, :], w2_raw[:, t, :], ACT.Copy, scale=gain_sign[:, t : t + 1])
         w2_grouped = keep.tile([P, N, PACK], BF16, name="w2_grouped", align_bytes=64)
@@ -197,7 +186,7 @@ def tile_picked_hashkind_none_p_kernel(
         nc.vector.tensor_tensor(smaller[:], first_nb[:, :, :HALF], second_nb[:], ALU.min)
         z_planes = keep.tile([P, PACK, HALF], BF16, name="z_planes", align_bytes=64)
         nc.vector.tensor_tensor(z_planes[:], smaller[:], rounded[:, :, :HALF], ALU.max)
-        z_grouped = stage.tile([P, HALF, PACK], BF16, name="z_grouped", offset=4 * U * 2, align_bytes=64)
+        z_grouped = keep.tile([P, HALF, PACK], BF16, name="z_grouped", tag="late_slot", align_bytes=64)
         nc.scalar.copy(*interleave_views(z_grouped[:], z_planes[:]))
         codes, scales = quantise(z_grouped, HALF, "early")
         for pair in range(2):
@@ -213,7 +202,7 @@ def tile_picked_hashkind_none_p_kernel(
             if pair == 0:
                 nb = keep.tile([P, 2, HALF], BF16, name="late_nb0", tag="early_slot", align_bytes=64)
             else:
-                nb = stage.tile([P, 2, HALF], BF16, name="late_nb1", offset=4 * U * 2, align_bytes=64)
+                nb = keep.tile([P, 2, HALF], BF16, name="late_nb1", tag="late_slot", align_bytes=64)
             for u in range(2):
                 nc.vector.tensor_copy(nb[:, u, :], scaled[2 * pair + u][:].indirect(entries(n2_sb, HALF, HALF)))
             planes = slice(2 * pair, 2 * pair + 2)

from contextlib import ExitStack

import concourse.mybir as mybir

K, T, S, N, H, U = 512, 2048, 512, 512, 512, 512
FLOPS = 2 * K * H * S + 2 * H * N * S

F32 = mybir.dt.float32
BF16 = mybir.dt.bfloat16
I32 = mybir.dt.int32
U32 = mybir.dt.uint32
U16 = mybir.dt.uint16
U8 = mybir.dt.uint8
FP8X4 = mybir.dt.float8_e4m3fn_x4
ALU = mybir.AluOpType
ACT = mybir.ActivationFunctionType

P = 128
PACK = 4
GROUP = 16
HALF = 256
CHUNKS = ((0, 256), (256, 256))


def tile_picked_hashkind_none_p_kernel(
    tc, x_words, x_scales, w1, tab, gn, w2, offs, kind, n1, n2, out
):
    nc = tc.nc
    with ExitStack() as ctx:
        lists = ctx.enter_context(tc.tile_pool(name="lists", bufs=1))
        keep = ctx.enter_context(tc.tile_pool(name="keep", bufs=1))
        psum = ctx.enter_context(tc.psum_pool(name="psum", bufs=1))

        def entries(tile, start, count):
            return tile[:, start // GROUP : (start + count) // GROUP]

        offs_sb = lists.tile([P, S // GROUP], U16, name="offs_sb")
        kind_sb = lists.tile([P, S // GROUP], U16, name="kind_sb")
        n1_sb = lists.tile([P, S // GROUP], U16, name="n1_sb")
        n2_sb = lists.tile([P, S // GROUP], U16, name="n2_sb")

        xs_win = keep.tile([P, T], U8, name="xs_win", align_bytes=64)

        nc.vector.memset(xs_win[:, : T // 2].bitcast(I32), 0)
        nc.gpsimd.memset(xs_win[:, T // 2 :].bitcast(I32), 0)
        scale_rows = x_scales[0].bitcast(I32).rearrange("(g e) c -> e g c", e=2)
        for e in range(2):
            nc.sync.dma_start(xs_win[e:P:GROUP, :].bitcast(I32), scale_rows[e])
        nc.sync.dma_start(offs_sb[:], offs)
        gain = keep.tile([P, PACK], F32, name="gain")
        nc.sync.dma_start(gain[:], gn.rearrange("(p t) o -> p (t o)", t=PACK))
        nc.sync.dma_start(kind_sb[:], kind)
        tab_planes = tab.rearrange("(p t) c -> t p c", t=PACK)

        def load_tab(t):
            win = keep.tile([P, 2 * U], F32, name=f"tab_win{t}")
            nc.sync.dma_start(win[:, U:], tab_planes[t])
            return win

        tab_win = [load_tab(t) for t in range(PACK)]
        w1_raw = keep.tile([P, PACK, H], F32, name="w1_raw")
        nc.sync.dma_start(w1_raw[:], w1.rearrange("(p j) c -> p j c", j=PACK))
        xw_win = keep.tile([P, T], U32, name="xw_win", tag="big_load", align_bytes=64)
        nc.sync.dma_start(xw_win[:].bitcast(I32), x_words[0].rearrange("p n t -> p (n t)").bitcast(I32))
        nc.sync.dma_start(n1_sb[:], n1)
        nc.sync.dma_start(n2_sb[:], n2)

        gain_abs = keep.tile([P, PACK], F32, name="gain_abs")
        nc.scalar.activation(gain_abs[:], gain[:], ACT.Abs)
        twice_nonneg = keep.tile([P, PACK], F32, name="twice_nonneg")
        gain_sign = keep.tile([P, PACK], F32, name="gain_sign")
        nc.gpsimd.tensor_scalar(twice_nonneg[:], gain[:], 0.0, 2.0, ALU.is_ge, ALU.mult)
        nc.gpsimd.tensor_scalar(gain_sign[:], twice_nonneg[:], 1.0, -1.0, ALU.mult, ALU.add)

        xs_picked = keep.tile([P, S], U8, name="xs_picked", align_bytes=64)
        nc.vector.tensor_copy(xs_picked[:], xs_win[:].indirect(offs_sb[:]))
        xs_plane = keep.tile([P, S], U8, name="xs_plane", align_bytes=64)
        nc.vector.tensor_copy(xs_plane[:].bitcast(I32), xs_picked[:].bitcast(I32))
        for e in range(2):
            nc.sync.dma_start(xs_plane[2 + e : P : 32, :].bitcast(I32), xs_picked[GROUP + e : P : 32, :].bitcast(I32))

        bx_win = [keep.tile([P, 2 * S], F32, name=f"bx_win{t}") for t in range(PACK)]

        def pick_shift(t):
            nc.scalar.activation(tab_win[t][:, :U], tab_win[t][:, U:], ACT.Copy, scale=gain_abs[:, t : t + 1])
            nc.vector.tensor_copy(bx_win[t][:, S:], tab_win[t][:].indirect(kind_sb[:]))

        for t in range(PACK):
            pick_shift(t)

        w1_view = w1_raw[:].rearrange("p j (m t) -> p m t j", t=PACK)
        w1_grouped = []
        for pair in range(2):
            grouped = keep.tile([P, 2, P, PACK], BF16, name=f"w1_grouped{pair}", align_bytes=64)
            nc.scalar.copy(grouped[:].rearrange("p t m j -> p m t j"), w1_view[:, :, 2 * pair : 2 * pair + 2, :])
            w1_grouped.append(grouped)

        def quantise_w1(pair, tag):
            codes = keep.tile([P, 2 * P], U32, name=f"w1_codes{pair}", tag=tag, align_bytes=64)
            scales = keep.tile([P, 2 * P], U8, name=f"w1_scales{pair}", align_bytes=64)
            nc.vector.quantize_mx(
                out=codes[:].bitcast(FP8X4), scales=scales[:], in_=w1_grouped[pair][:].rearrange("p t m j -> p (t m j)")
            )
            return codes, scales

        w1_mx = [quantise_w1(0, "w1_codes0")]
        xw_picked = keep.tile([P, S], U32, name="xw_picked", align_bytes=64)
        nc.vector.tensor_copy(xw_picked[:], xw_win[:].indirect(offs_sb[:]))
        w1_mx.append(quantise_w1(1, "big_load"))
        w2_raw = keep.tile([P, PACK, N], F32, name="w2_raw", tag="xs_picked", align_bytes=64)
        nc.sync.dma_start(w2_raw[:], w2.rearrange("(p j) c -> p j c", j=PACK))

        rounded = keep.tile([P, PACK, S], BF16, name="rounded", align_bytes=64)
        for t in range(PACK):
            bank = psum.tile([P, S], F32, name=f"y_bank{t // 2}{t % 2}")
            cols = slice(P * (t % 2), P * (t % 2 + 1))
            nc.tensor.matmul_mx(
                out=bank[:],
                lhsT=w1_mx[t // 2][0][:, cols].bitcast(FP8X4),
                lhsT_scale=w1_mx[t // 2][1][:, cols],
                rhs=xw_picked[:].bitcast(FP8X4),
                rhs_scale=xs_plane[:],
                start=True,
                stop=True,
            )
            if t == 0:
                nc.vector.scalar_tensor_tensor(
                    bx_win[t][:, :S], bank[:], gain_abs[:, t : t + 1], bx_win[t][:, S:], ALU.mult, ALU.add
                )
            else:
                y = keep.tile([P, S], F32, name=f"y{t}")
                nc.scalar.activation(y[:], bank[:], ACT.Copy, scale=gain_abs[:, t : t + 1])
                nc.gpsimd.tensor_tensor(bx_win[t][:, :S], y[:], bx_win[t][:, S:], ALU.add)
        scaled = bx_win
        for t in range(PACK):
            nc.scalar.copy(rounded[:, t, :], scaled[t][:, :S])

        w2_signed = keep.tile([P, PACK, N], BF16, name="w2_signed", tag="late_slot", align_bytes=64)
        for t in range(PACK):
            nc.scalar.activation(w2_signed[:, t, :], w2_raw[:, t, :], ACT.Copy, scale=gain_sign[:, t : t + 1])
        w2_grouped = keep.tile([P, N, PACK], BF16, name="w2_grouped", align_bytes=64)
        nc.scalar.copy(
            w2_grouped[:].rearrange("p (c i) t -> p c t i", i=4),
            w2_signed[:].rearrange("p t (c i) -> p c t i", i=4),
        )
        w2_codes = keep.tile([P, N], U32, name="w2_codes", align_bytes=64)
        w2_scales = keep.tile([P, N], U8, name="w2_scales", align_bytes=64)
        nc.vector.quantize_mx(
            out=w2_codes[:].bitcast(FP8X4), scales=w2_scales[:], in_=w2_grouped[:].rearrange("p n t -> p (n t)")
        )

        out_view = out.rearrange("(a p) j -> p a j", p=P)

        def quantise(grouped, count, label):
            codes = keep.tile([P, count], U32, name=f"z_codes{label}", align_bytes=64)
            scales = keep.tile([P, count], U8, name=f"z_scales{label}", align_bytes=64)
            nc.vector.quantize_mx(
                out=codes[:].bitcast(FP8X4), scales=scales[:], in_=grouped[:].rearrange("p n t -> p (n t)")
            )
            return codes, scales

        def second_product(codes, scales, pair, bank):
            for u in range(2):
                cols = slice(P * (2 * pair + u), P * (2 * pair + u + 1))
                nc.tensor.matmul_mx(
                    out=bank[:, u, :],
                    lhsT=w2_codes[:, cols].bitcast(FP8X4),
                    lhsT_scale=w2_scales[:, cols],
                    rhs=codes[:].bitcast(FP8X4),
                    rhs_scale=scales[:],
                    start=True,
                    stop=True,
                )

        def interleave_views(grouped, planes):
            return grouped.rearrange("p (c i) t -> p c t i", i=4), planes.rearrange("p t (c i) -> p c t i", i=4)

        first_nb = keep.tile([P, PACK, S], BF16, name="first_nb", align_bytes=64)
        for t in range(PACK):
            nc.vector.tensor_copy(first_nb[:, t, :], scaled[t][:].indirect(n1_sb[:]))

        second_nb = keep.tile([P, PACK, HALF], BF16, name="second_nb", align_bytes=64)
        for t in range(PACK):
            nc.vector.tensor_copy(second_nb[:, t, :], scaled[t][:].indirect(entries(n2_sb, 0, HALF)))
        smaller = keep.tile([P, PACK, HALF], BF16, name="smaller", tag="early_slot", align_bytes=64)
        nc.vector.tensor_tensor(smaller[:], first_nb[:, :, :HALF], second_nb[:], ALU.min)
        z_planes = keep.tile([P, PACK, HALF], BF16, name="z_planes", align_bytes=64)
        nc.vector.tensor_tensor(z_planes[:], smaller[:], rounded[:, :, :HALF], ALU.max)
        z_grouped = keep.tile([P, HALF, PACK], BF16, name="z_grouped", tag="late_slot", align_bytes=64)
        nc.scalar.copy(*interleave_views(z_grouped[:], z_planes[:]))
        codes, scales = quantise(z_grouped, HALF, "early")
        for pair in range(2):
            bank = psum.tile([P, 2, HALF], F32, name=f"out_bank{pair}")
            second_product(codes, scales, pair, bank)
            result = keep.tile([P, 2, HALF], F32, name=f"result{pair}")
            nc.scalar.copy(result[:], bank[:])
            nc.sync.dma_start(out_view[:, 2 * pair : 2 * pair + 2, :HALF], result[:])

        smaller_late = keep.tile([P, PACK, HALF], BF16, name="smaller_late", align_bytes=64)
        z_late = keep.tile([P, PACK, HALF], BF16, name="z_late", align_bytes=64)
        for pair in range(2):
            if pair == 0:
                nb = keep.tile([P, 2, HALF], BF16, name="late_nb0", tag="early_slot", align_bytes=64)
            else:
                nb = keep.tile([P, 2, HALF], BF16, name="late_nb1", tag="late_slot", align_bytes=64)
            for u in range(2):
                nc.vector.tensor_copy(nb[:, u, :], scaled[2 * pair + u][:].indirect(entries(n2_sb, HALF, HALF)))
            planes = slice(2 * pair, 2 * pair + 2)
            nc.vector.tensor_tensor(smaller_late[:, planes, :], first_nb[:, planes, HALF:], nb[:], ALU.min)
        nc.vector.tensor_tensor(z_late[:], smaller_late[:], rounded[:, :, HALF:], ALU.max)
        quarter = HALF // 2
        for q in range(2):
            grouped = keep.tile([P, quarter, PACK], BF16, name=f"z_grouped_late{q}", align_bytes=64)
            views = interleave_views(grouped[:], z_late[:, :, q * quarter : (q + 1) * quarter])
            if q == 0:
                nc.vector.tensor_copy(*views)
            else:
                nc.scalar.copy(*views)
            codes, scales = quantise(grouped, quarter, f"late{q}")
            result = keep.tile([P, PACK, quarter], F32, name=f"result_late{q}")
            for pair in range(2):
                bank = psum.tile([P, 2, quarter], F32, name=f"late_bank{q}{pair}", tag=f"y_bank{q}{pair}")
                second_product(codes, scales, pair, bank)
                if pair == 0:
                    nc.scalar.copy(result[:, :2, :], bank[:])
                else:
                    nc.vector.tensor_copy(result[:, 2:, :], bank[:])
            start = HALF + q * quarter
            nc.sync.dma_start(out_view[:, :, start : start + quarter], result[:])
